import numpy as np
import ml_dtypes


def mxq(x, axis, fmt="e4m3"):
    dtype, down = {"e4m3": (ml_dtypes.float8_e4m3fn, 7), "e5m2": (ml_dtypes.float8_e5m2, 14)}[fmt]
    v = np.moveaxis(np.asarray(x, np.float32).astype(ml_dtypes.bfloat16).astype(np.float64), axis, -1)
    blocks = v.reshape(v.shape[:-1] + (-1, 32))
    amax = np.abs(blocks).max(-1, keepdims=True)
    byte = np.maximum(np.where(amax > 0, np.frexp(amax)[1] - 1 + 127, 0) - down, 1)
    scale = np.exp2(byte - 127.0)
    codes = (blocks / scale).astype(np.float32).astype(dtype).astype(np.float64)
    return np.moveaxis((codes * scale).reshape(v.shape), -1, axis)


WIDE = False


def mx_kscale(k):
    if not WIDE:
        return np.ones(k)
    levels = np.array([10, -10, 5, -5, 0])
    if k % 512:
        return np.exp2(np.random.permutation(np.resize(levels, k // 32))).repeat(32)
    a = np.empty((k // 512, 16))
    for p in range(k // 512):
        a[p, :8] = np.random.permutation(np.resize(levels, 8))
        for g in range(8):
            far = levels[np.abs(levels - a[p, g]) >= 10]
            a[p, g + 8] = far[np.random.randint(len(far))]
    return np.exp2(a.ravel()).repeat(32)


def f64(x):
    return np.asarray(x).astype(np.float64)


def striped(idx):
    return np.tile(idx.reshape(-1, 16).T, (8, 1)).astype(np.uint16)


def unstriped(offs):
    return offs[:16].T.reshape(-1).astype(np.int64)


def pack_weight(w):
    k, n = w.shape
    w = f64(np.asarray(w, np.float32).astype(ml_dtypes.bfloat16)).reshape(k // 32, 32, n)
    amax = np.abs(w).max(1)
    byte = np.clip(np.where(amax > 0, np.frexp(amax)[1] - 1 + 127 - 7, 1), 1, 254)
    scaled = (w * np.exp2(127.0 - byte)[:, None, :]).reshape(k, n).astype(np.float32)
    words = np.ascontiguousarray(scaled.reshape(k // 512, 128, 4, n).transpose(0, 1, 3, 2)).astype(ml_dtypes.float8_e4m3fn).view(np.uint8)
    return words, np.ascontiguousarray(byte.astype(np.uint8).reshape(k // 512, 16, n))


def unpack_weight(words, scales):
    g, p, n, _ = words.shape
    vals = np.ascontiguousarray(words).view(ml_dtypes.float8_e4m3fn).astype(np.float64) * np.repeat(np.exp2(scales.astype(np.float64) - 127.0), 8, axis=1)[..., None]
    return vals.transpose(0, 1, 3, 2).reshape(g * 512, n)

def planes(y):
    n, m = y.shape
    v = y.astype(np.float32).astype(ml_dtypes.bfloat16).astype(np.float64).reshape(n // 32, 32, m)
    top = np.abs(v).max(1)
    byte = np.clip(np.where(top > 0, np.frexp(top)[1] - 1 + 127 - 7, 1), 1, 254)
    codes = (v * np.exp2(127.0 - byte)[:, None, :]).reshape(n, m).astype(np.float32).astype(ml_dtypes.float8_e4m3fn).view(np.uint8)
    words = codes.reshape(n // 512, 128, 4, m).transpose(0, 1, 3, 2)
    return np.ascontiguousarray(words), np.ascontiguousarray(byte.astype(np.uint8).reshape(n // 512, 16, m))


K, T, S, N, H, W = 512, 2048, 512, 512, 512, 1024


def setup_inputs():
    n = np.random.standard_normal
    s = mx_kscale(K)[:, None]
    u = mx_kscale(H)
    packed_xT = pack_weight(n((K, T)) * s)
    packed_w1 = pack_weight(n((K, H)) / np.sqrt(K) / s)
    packed_w2 = pack_weight(n((H, N)) / np.sqrt(2 * H) / u[:, None])
    packed_w3 = pack_weight(n((K, N)) / np.sqrt(2 * K) / s)
    return {
        "x_words": packed_xT[0],
        "x_scales": packed_xT[1],
        "w1_words": packed_w1[0],
        "w1_scales": packed_w1[1],
        "gn": (np.random.uniform(0.5, 1.5, (H, 1)) * u[:, None]).astype(np.float32),
        "w2_words": packed_w2[0],
        "w2_scales": packed_w2[1],
        "w3_words": packed_w3[0],
        "w3_scales": packed_w3[1],
        "offs": striped(np.random.permutation(T)[:S]),
        "n1": striped(np.random.permutation(S)),
        "n2": striped(np.random.permutation(S)),
        "two": striped(np.random.permutation(T)[:S]),
        "n3": striped(np.random.randint(0, S, W)),
        "n4": striped(np.random.permutation(S)),
    }


def reference(x_words, x_scales, w1_words, w1_scales, gn, w2_words, w2_scales, w3_words, w3_scales, offs, n1, n2, two, n3, n4):
    xq = unpack_weight(x_words, x_scales)[:, unstriped(offs)]
    y = unpack_weight(w1_words, w1_scales).T @ xq
    z = f64(gn) * ((y * y[:, unstriped(n1)]) * (np.tanh(y[:, unstriped(n2)])))
    x_two = unpack_weight(x_words, x_scales)[:, unstriped(two)]
    h = unpack_weight(w2_words, w2_scales).T @ mxq(z, 0, "e4m3") + unpack_weight(w3_words, w3_scales).T @ x_two
    mb = h[:, unstriped(n3)]
    mx = mb.reshape(N, S, 2).max(axis=2)
    st = h - mx
    out_0 = np.maximum(st, st[:, unstriped(n4)])
    return (out_0,) + planes(out_0)

@@ -1,0 +1,209 @@
+from contextlib import ExitStack
+
+import concourse.mybir as mybir
+
+K, T, S, H, N = 512, 2048, 512, 512, 512
+FLOPS = 2 * S * (K * H + H * N + K * N)
+
+F32 = mybir.dt.float32
+BF16 = mybir.dt.bfloat16
+I32 = mybir.dt.int32
+U32 = mybir.dt.uint32
+U16 = mybir.dt.uint16
+U8 = mybir.dt.uint8
+FP8X4 = mybir.dt.float8_e4m3fn_x4
+ALU = mybir.AluOpType
+ACT = mybir.ActivationFunctionType
+
+P = 128
+PACK = 4
+QUADS = 4
+HALF = S // 2
+SPARE = 16
+
+
+def tile_picked_mixincubeghopm_none_po_kernel(
+    tc, x_words, x_scales, w1_words, w1_scales, gn, w2_words, w2_scales, w3_words, w3_scales,
+    offs, n1, n2, two, n3, n4, out_0, out_1, out_2,
+):
+    nc = tc.nc
+    with ExitStack() as ctx:
+        sb = ctx.enter_context(tc.tile_pool(name="sb", bufs=1))
+        ps = ctx.enter_context(tc.psum_pool(name="ps", bufs=1))
+
+        def load_list(src, name):
+            tile = sb.tile(list(src.shape), U16, name=name)
+            nc.sync.dma_start(tile[:], src)
+            return tile
+
+        def load_words(src, name):
+            tile = sb.tile([P, src.shape[2]], U32, name=name, tag=name, align_bytes=64)
+            nc.sync.dma_start(tile[:].bitcast(I32), src[0].rearrange("p n t -> p (n t)").bitcast(I32))
+            return tile
+
+        def load_scales(src, name, queues):
+            tile = sb.tile([P, src.shape[2]], U8, name=name, align_bytes=64)
+            for q in range(QUADS):
+                rows = src[0, 4 * q : 4 * q + 4, :].bitcast(I32)
+                queues[q].dma_start(tile[32 * q : 32 * q + 32, :].bitcast(I32), rows.partition_broadcast(8))
+            return tile
+
+        def load_scale_pair(first, second, name):
+            tile = sb.tile([P, first.shape[2]], U8, name=name, align_bytes=64)
+            nc.gpsimd.memset(tile[:].bitcast(I32), 0)
+            for k, src in ((0, first), (4, second)):
+                for q in range(QUADS):
+                    rows = src[0, 4 * q : 4 * q + 4, :].bitcast(I32)
+                    nc.sync.dma_start(tile[32 * q + k : 32 * q + k + 4, :].bitcast(I32), rows)
+            return tile
+
+        def deal(raw, name, view):
+            tile = sb.tile([P, raw.shape[1]], raw.dtype, name=name, align_bytes=64)
+            nc.vector.tensor_copy(
+                tile[:].bitcast(view).rearrange("p (t m) -> p t m", t=PACK),
+                raw[:].bitcast(view).rearrange("p (m t) -> p t m", t=PACK),
+            )
+            return tile
+
+        def gather_tokens(table, lst, dtype, name, tag=None):
+            tile = sb.tile([P, S], dtype, name=name, tag=tag or name, align_bytes=64)
+            nc.vector.tensor_copy(tile[:], table[:].indirect(lst[:]))
+            return tile
+
+        def window(name):
+            tile = sb.tile([P, S + SPARE], F32, name=name)
+            nc.gpsimd.memset(tile[:, S:], 0.0)
+            return tile
+
+        def cols(c):
+            return slice(c * HALF, (c + 1) * HALF)
+
+        def entries(lst, piece, count):
+            return lst[:, piece * count // 16 : (piece + 1) * count // 16]
+
+        def round_and_quantize(planes, grouped, codes, scales):
+            nc.vector.tensor_copy(
+                grouped[:].rearrange("p (c i) t -> p c t i", i=4),
+                planes[:].rearrange("p t (c i) -> p c t i", i=4),
+            )
+            nc.vector.quantize_mx(out=codes.bitcast(FP8X4), scales=scales, in_=grouped[:].rearrange("p j t -> p (j t)"))
+
+        xs = load_scales(x_scales, "xs", (nc.sync, nc.scalar, nc.sync, nc.scalar))
+        offs_t = load_list(offs, "offs_t")
+        two_t = load_list(two, "two_t")
+        xw = load_words(x_words, "xw")
+        w1_raw = load_words(w1_words, "w1_raw")
+        w1s_raw = load_scales(w1_scales, "w1s_raw", (nc.scalar,) * QUADS)
+        n2_t = load_list(n2, "n2_t")
+        n1_t = load_list(n1, "n1_t")
+        gain = sb.tile([P, PACK], F32, name="gain")
+        nc.sync.dma_start(gain[:], gn.rearrange("(p t) o -> p (t o)", t=PACK))
+        w3_raw = load_words(w3_words, "w3_raw")
+        w2_raw = load_words(w2_words, "w2_raw")
+        w32s_raw = load_scale_pair(w3_scales, w2_scales, "w32s_raw")
+        n3_t = load_list(n3, "n3_t")
+        n4_t = load_list(n4, "n4_t")
+
+        tanh_y = [window(f"tanh_y{t}") for t in range(PACK)]
+        h = [window(f"h{t}") for t in range(PACK)]
+
+        xq_s = gather_tokens(xs, offs_t, U8, "xq_s")
+        x2_s = gather_tokens(xs, two_t, U8, "x2_s")
+        w1s = deal(w1s_raw, "w1s", U8)
+        xq = gather_tokens(xw, offs_t, U32, "xq")
+        w1 = deal(w1_raw, "w1", I32)
+
+        def mm(out, w, ws, k, t, rhs, rhs_s, start, stop):
+            m = slice(t * P, (t + 1) * P)
+            nc.tensor.matmul_mx(
+                out=out, lhsT=w[:, m].bitcast(FP8X4), lhsT_scale=ws[k:, m],
+                rhs=rhs.bitcast(FP8X4), rhs_scale=rhs_s, start=start, stop=stop,
+            )
+
+        y_ps = [ps.tile([P, S], F32, name=f"y_ps{t}", tag=f"late{t}") for t in range(PACK)]
+        for t in range(PACK):
+            mm(y_ps[t][:], w1, w1s, 0, t, xq[:], xq_s[:], True, True)
+
+        x2 = gather_tokens(xw, two_t, U32, "x2", tag="w1_raw")
+        w3 = deal(w3_raw, "w3", I32)
+        w2 = deal(w2_raw, "w2", I32)
+        w32s = deal(w32s_raw, "w32s", U8)
+
+        y = [sb.tile([P, S], F32, name=f"y{t}") for t in range(PACK)]
+        b = [sb.tile([P, S], F32, name=f"b{t}") for t in range(PACK)]
+        for t in range(PACK):
+            nc.scalar.activation(tanh_y[t][:, :S], y_ps[t][:], ACT.Tanh)
+            nc.scalar.activation(y[t][:], y_ps[t][:], ACT.Copy)
+            nc.vector.tensor_tensor(b[t][:], tanh_y[t][:].indirect(n2_t[:]), y[t][:], ALU.mult)
+
+        h_ps = [[ps.tile([P, HALF], F32, name=f"h_ps{t}_{c}", tag=("early", "late")[c] + str(t)) for c in range(2)] for t in range(PACK)]
+        for c in range(2):
+            for t in range(PACK):
+                mm(h_ps[t][c][:], w3, w32s, 0, t, x2[:, cols(c)], x2_s[:, cols(c)], True, False)
+
+        for c in range(2):
+            z = sb.tile([P, PACK, HALF], F32, name=f"z{c}")
+            for t in range(PACK):
+                y_n1 = sb.tile([P, HALF], F32, name=f"y_n1_{t}_{c}")
+                nc.scalar.activation(y_n1[:], y[t][:].indirect(entries(n1_t, c, HALF)), ACT.Copy)
+                nc.vector.scalar_tensor_tensor(z[:, t, :], b[t][:, cols(c)], gain[:, t : t + 1], y_n1[:], ALU.mult, ALU.mult)
+            z_grouped = sb.tile([P, HALF, PACK], BF16, name=f"z_grouped{c}", align_bytes=64)
+            zq = sb.tile([P, HALF], U32, name=f"zq{c}", align_bytes=64)
+            zq_s = sb.tile([P, HALF], U8, name=f"zq_s{c}", align_bytes=64)
+            round_and_quantize(z, z_grouped, zq[:], zq_s[:])
+            for t in range(PACK):
+                mm(h_ps[t][c][:], w2, w32s, 4, t, zq[:], zq_s[:], False, True)
+            for t in range(PACK):
+                if c == 0 or t == 0:
+                    nc.scalar.activation(h[t][:, cols(c)], h_ps[t][c][:], ACT.Copy)
+                else:
+                    nc.vector.tensor_copy(h[t][:, cols(c)], h_ps[t][c][:])
+
+        res = [sb.tile([P, PACK, HALF], F32, name=f"res{c}") for c in range(2)]
+        st = [sb.tile([P, S], F32, name=f"st{t}") for t in range(PACK)]
+        st_n4 = [[sb.tile([P, HALF], F32, name=f"st_n4_{t}_{c}") for c in range(2)] for t in range(PACK)]
+        mx = [[sb.tile([P, HALF], F32, name=f"mx{t}_{c}") for c in range(2)] for t in range(PACK)]
+        out_rows = out_0.rearrange("(p t) j -> p t j", t=PACK)
+
+        def members(t, c):
+            mb = sb.tile([P, HALF, 2], F32, name=f"mb{t}_{c}")
+            nc.scalar.activation(mb[:].rearrange("p j m -> p (j m)"), h[t][:].indirect(entries(n3_t, c, S)), ACT.Copy)
+            nc.vector.tensor_tensor(mx[t][c][:], mb[:, :, 0], mb[:, :, 1], ALU.max)
+
+        def subtract(t, c):
+            nc.vector.tensor_tensor(st[t][:, cols(c)], h[t][:, cols(c)], mx[t][c][:], ALU.subtract)
+
+        def fetch_n4(t, c):
+            looked_up = st[t][:].indirect(entries(n4_t, c, HALF))
+            if t < 2:
+                nc.vector.tensor_copy(st_n4[t][c][:], looked_up)
+            else:
+                nc.scalar.activation(st_n4[t][c][:], looked_up, ACT.Copy)
+
+        def finish(t, c):
+            nc.vector.tensor_tensor(res[c][:, t, :], st[t][:, cols(c)], st_n4[t][c][:], ALU.max)
+            nc.sync.dma_start(out_rows[:, t, cols(c)], res[c][:, t, :])
+
+        for t in range(PACK):
+            for c in range(2):
+                members(t, c)
+                if 1 <= t <= 2:
+                    fetch_n4(t - 1, c)
+                subtract(t, c)
+            if 1 <= t <= 2:
+                for c in range(2):
+                    finish(t - 1, c)
+        out_s = sb.tile([P, S], U8, name="out_s", align_bytes=64)
+        for t in (2, 3):
+            for c in range(2):
+                fetch_n4(t, c)
+                finish(t, c)
+                if t == 3:
+                    grouped = sb.tile([P, HALF, PACK], BF16, name=f"res_grouped{c}", align_bytes=64)
+                    codes = sb.tile([P, HALF], U32, name=f"out_w{c}", align_bytes=64)
+                    round_and_quantize(res[c], grouped, codes[:], out_s[:, cols(c)])
+                    words = out_1[0].rearrange("p n t -> p (n t)").bitcast(I32)
+                    nc.sync.dma_start(words[:, cols(c)], codes[:].bitcast(I32))
+        for q in range(QUADS):
+            queue = (nc.sync, nc.scalar)[q % 2]
+            queue.dma_start(out_2[0, 4 * q : 4 * q + 4, :].bitcast(I32), out_s[32 * q : 32 * q + 4, :].bitcast(I32))

@@ -36,9 +36,9 @@ def tile_picked_mixincubeghopm_none_po_kernel(
             nc.sync.dma_start(tile[:], src)
             return tile
 
-        def load_words(src, name):
+        def load_words(src, name, queue):
             tile = sb.tile([P, src.shape[2]], U32, name=name, tag=name, align_bytes=64)
-            nc.sync.dma_start(tile[:].bitcast(I32), src[0].rearrange("p n t -> p (n t)").bitcast(I32))
+            queue.dma_start(tile[:].bitcast(I32), src[0].rearrange("p n t -> p (n t)").bitcast(I32))
             return tile
 
         def load_scales(src, name, queues):
@@ -60,8 +60,8 @@ def tile_picked_mixincubeghopm_none_po_kernel(
         def deal(raw, name, view):
             tile = sb.tile([P, raw.shape[1]], raw.dtype, name=name, align_bytes=64)
             nc.vector.tensor_copy(
-                tile[:].bitcast(view).rearrange("p (t m) -> p t m", t=PACK),
-                raw[:].bitcast(view).rearrange("p (m t) -> p t m", t=PACK),
+                tile[:].bitcast(view).rearrange("p (t c i) -> p c t i", t=PACK, i=4),
+                raw[:].bitcast(view).rearrange("p (c i t) -> p c t i", t=PACK, i=4),
             )
             return tile
 
@@ -81,25 +81,27 @@ def tile_picked_mixincubeghopm_none_po_kernel(
         def entries(lst, piece, count):
             return lst[:, piece * count // 16 : (piece + 1) * count // 16]
 
-        def round_and_quantize(planes, grouped, codes, scales):
-            nc.vector.tensor_copy(
-                grouped[:].rearrange("p (c i) t -> p c t i", i=4),
-                planes[:].rearrange("p t (c i) -> p c t i", i=4),
-            )
+        def walk_planes(planes):
+            return planes.rearrange("p t (c i) -> p c t i", i=4)
+
+        def walk_grouped(grouped):
+            return grouped[:].rearrange("p (c i) t -> p c t i", i=4)
+
+        def quantize(grouped, codes, scales):
             nc.vector.quantize_mx(out=codes.bitcast(FP8X4), scales=scales, in_=grouped[:].rearrange("p j t -> p (j t)"))
 
-        xs = load_scales(x_scales, "xs", (nc.sync, nc.scalar, nc.sync, nc.scalar))
         offs_t = load_list(offs, "offs_t")
         two_t = load_list(two, "two_t")
-        xw = load_words(x_words, "xw")
-        w1_raw = load_words(w1_words, "w1_raw")
-        w1s_raw = load_scales(w1_scales, "w1s_raw", (nc.scalar,) * QUADS)
+        xs = load_scales(x_scales, "xs", (nc.scalar, nc.scalar, nc.scalar, nc.sync))
+        xw = load_words(x_words, "xw", nc.scalar)
+        w1s_raw = load_scales(w1_scales, "w1s_raw", (nc.sync,) * QUADS)
+        w1_raw = load_words(w1_words, "w1_raw", nc.sync)
         n2_t = load_list(n2, "n2_t")
         n1_t = load_list(n1, "n1_t")
         gain = sb.tile([P, PACK], F32, name="gain")
         nc.sync.dma_start(gain[:], gn.rearrange("(p t) o -> p (t o)", t=PACK))
-        w3_raw = load_words(w3_words, "w3_raw")
-        w2_raw = load_words(w2_words, "w2_raw")
+        w3_raw = load_words(w3_words, "w3_raw", nc.sync)
+        w2_raw = load_words(w2_words, "w2_raw", nc.sync)
         w32s_raw = load_scale_pair(w3_scales, w2_scales, "w32s_raw")
         n3_t = load_list(n3, "n3_t")
         n4_t = load_list(n4, "n4_t")
@@ -130,40 +132,56 @@ def tile_picked_mixincubeghopm_none_po_kernel(
         w32s = deal(w32s_raw, "w32s", U8)
 
         y = [sb.tile([P, S], F32, name=f"y{t}") for t in range(PACK)]
-        b = [sb.tile([P, S], F32, name=f"b{t}") for t in range(PACK)]
+        b = sb.tile([P, PACK, S], F32, name="b")
         for t in range(PACK):
             nc.scalar.activation(tanh_y[t][:, :S], y_ps[t][:], ACT.Tanh)
             nc.scalar.activation(y[t][:], y_ps[t][:], ACT.Copy)
-            nc.vector.tensor_tensor(b[t][:], tanh_y[t][:].indirect(n2_t[:]), y[t][:], ALU.mult)
+            nc.vector.tensor_tensor(b[:, t, :], tanh_y[t][:].indirect(n2_t[:]), y[t][:], ALU.mult)
 
         h_ps = [[ps.tile([P, HALF], F32, name=f"h_ps{t}_{c}", tag=("early", "late")[c] + str(t)) for c in range(2)] for t in range(PACK)]
         for c in range(2):
             for t in range(PACK):
                 mm(h_ps[t][c][:], w3, w32s, 0, t, x2[:, cols(c)], x2_s[:, cols(c)], True, False)
 
-        for c in range(2):
-            z = sb.tile([P, PACK, HALF], F32, name=f"z{c}")
-            for t in range(PACK):
-                y_n1 = sb.tile([P, HALF], F32, name=f"y_n1_{t}_{c}")
-                nc.scalar.activation(y_n1[:], y[t][:].indirect(entries(n1_t, c, HALF)), ACT.Copy)
-                nc.vector.scalar_tensor_tensor(z[:, t, :], b[t][:, cols(c)], gain[:, t : t + 1], y_n1[:], ALU.mult, ALU.mult)
-            z_grouped = sb.tile([P, HALF, PACK], BF16, name=f"z_grouped{c}", align_bytes=64)
+        z = [sb.tile([P, PACK, HALF], F32, name=f"z{c}") for c in range(2)]
+        z_grouped = [sb.tile([P, HALF, PACK], BF16, name=f"z_grouped{c}", align_bytes=64) for c in range(2)]
+
+        def make_z(t, c):
+            y_n1 = sb.tile([P, HALF], F32, name=f"y_n1_{t}_{c}")
+            nc.scalar.activation(y_n1[:], y[t][:].indirect(entries(n1_t, c, HALF)), ACT.Copy)
+            nc.vector.scalar_tensor_tensor(z[c][:, t, :], b[:, t, cols(c)], gain[:, t : t + 1], y_n1[:], ALU.mult, ALU.mult)
+
+        def round_z(c):
+            nc.vector.tensor_copy(walk_grouped(z_grouped[c]), walk_planes(z[c][:]))
+
+        def second_product(c):
             zq = sb.tile([P, HALF], U32, name=f"zq{c}", align_bytes=64)
             zq_s = sb.tile([P, HALF], U8, name=f"zq_s{c}", align_bytes=64)
-            round_and_quantize(z, z_grouped, zq[:], zq_s[:])
+            quantize(z_grouped[c], zq[:], zq_s[:])
             for t in range(PACK):
                 mm(h_ps[t][c][:], w2, w32s, 4, t, zq[:], zq_s[:], False, True)
-            for t in range(PACK):
-                if c == 0 or t == 0:
-                    nc.scalar.activation(h[t][:, cols(c)], h_ps[t][c][:], ACT.Copy)
-                else:
-                    nc.vector.tensor_copy(h[t][:, cols(c)], h_ps[t][c][:])
 
-        res = [sb.tile([P, PACK, HALF], F32, name=f"res{c}") for c in range(2)]
+        for t in range(PACK):
+            make_z(t, 0)
+        make_z(0, 1)
+        round_z(0)
+        make_z(1, 1)
+        second_product(0)
+        make_z(2, 1)
+        make_z(3, 1)
+        for t in range(PACK):
+            nc.scalar.activation(h[t][:, cols(0)], h_ps[t][0][:], ACT.Copy)
+        round_z(1)
+        second_product(1)
+        nc.scalar.activation(h[0][:, cols(1)], h_ps[0][1][:], ACT.Copy)
+        for t in range(1, PACK):
+            nc.vector.tensor_copy(h[t][:, cols(1)], h_ps[t][1][:])
+
+        res = sb.tile([P, 2, PACK, HALF], F32, name="res")
         st = [sb.tile([P, S], F32, name=f"st{t}") for t in range(PACK)]
-        st_n4 = [[sb.tile([P, HALF], F32, name=f"st_n4_{t}_{c}") for c in range(2)] for t in range(PACK)]
+        st_n4 = [sb.tile([P, S], F32, name=f"st_n4_{t}") for t in range(PACK)]
         mx = [[sb.tile([P, HALF], F32, name=f"mx{t}_{c}") for c in range(2)] for t in range(PACK)]
-        out_rows = out_0.rearrange("(p t) j -> p t j", t=PACK)
+        out_rows = out_0.rearrange("(p t) (c j) -> p c t j", t=PACK, c=2)
 
         def members(t, c):
             mb = sb.tile([P, HALF, 2], F32, name=f"mb{t}_{c}")
@@ -176,34 +194,62 @@ def tile_picked_mixincubeghopm_none_po_kernel(
         def fetch_n4(t, c):
             looked_up = st[t][:].indirect(entries(n4_t, c, HALF))
             if t < 2:
-                nc.vector.tensor_copy(st_n4[t][c][:], looked_up)
+                nc.vector.tensor_copy(st_n4[t][:, cols(c)], looked_up)
             else:
-                nc.scalar.activation(st_n4[t][c][:], looked_up, ACT.Copy)
+                nc.scalar.activation(st_n4[t][:, cols(c)], looked_up, ACT.Copy)
 
         def finish(t, c):
-            nc.vector.tensor_tensor(res[c][:, t, :], st[t][:, cols(c)], st_n4[t][c][:], ALU.max)
-            nc.sync.dma_start(out_rows[:, t, cols(c)], res[c][:, t, :])
+            nc.vector.tensor_tensor(res[:, c, t, :], st[t][:, cols(c)], st_n4[t][:, cols(c)], ALU.max)
+            if c == 1 or t == 3:
+                halves = slice(c, c + 1) if t == 3 else slice(0, 2)
+                nc.sync.dma_start(out_rows[:, halves, t, :], res[:, halves, t, :])
 
-        for t in range(PACK):
-            for c in range(2):
-                members(t, c)
-                if 1 <= t <= 2:
-                    fetch_n4(t - 1, c)
-                subtract(t, c)
-            if 1 <= t <= 2:
-                for c in range(2):
-                    finish(t - 1, c)
+        def finish_whole(t):
+            halves = "p (c j) -> p c j"
+            nc.vector.tensor_tensor(res[:, :, t, :], st[t][:].rearrange(halves, c=2), st_n4[t][:].rearrange(halves, c=2), ALU.max)
+            nc.sync.dma_start(out_rows[:, :, t, :], res[:, :, t, :])
+
         out_s = sb.tile([P, S], U8, name="out_s", align_bytes=64)
-        for t in (2, 3):
-            for c in range(2):
-                fetch_n4(t, c)
-                finish(t, c)
-                if t == 3:
-                    grouped = sb.tile([P, HALF, PACK], BF16, name=f"res_grouped{c}", align_bytes=64)
-                    codes = sb.tile([P, HALF], U32, name=f"out_w{c}", align_bytes=64)
-                    round_and_quantize(res[c], grouped, codes[:], out_s[:, cols(c)])
-                    words = out_1[0].rearrange("p n t -> p (n t)").bitcast(I32)
-                    nc.sync.dma_start(words[:, cols(c)], codes[:].bitcast(I32))
+        grouped = [sb.tile([P, HALF, PACK], BF16, name=f"res_grouped{c}", align_bytes=64) for c in range(2)]
+        codes = [sb.tile([P, HALF], U32, name=f"out_w{c}", align_bytes=64) for c in range(2)]
+        words = out_1[0].rearrange("p n t -> p (n t)").bitcast(I32)
+
+        def hand_on(c):
+            quantize(grouped[c], codes[c][:], out_s[:, cols(c)])
+            nc.sync.dma_start(words[:, cols(c)], codes[c][:].bitcast(I32))
+
+        for c in range(2):
+            members(0, c)
+            subtract(0, c)
+        fetch_n4(0, 0)
+        members(1, 0)
+        fetch_n4(0, 1)
+        subtract(1, 0)
+        members(1, 1)
+        finish_whole(0)
+        subtract(1, 1)
+        members(2, 0)
+        fetch_n4(1, 0)
+        subtract(2, 0)
+        fetch_n4(1, 1)
+        members(2, 1)
+        members(3, 0)
+        subtract(2, 1)
+        subtract(3, 0)
+        members(3, 1)
+        finish(1, 0)
+        subtract(3, 1)
+        finish(1, 1)
+        for c in range(2):
+            fetch_n4(2, c)
+        finish_whole(2)
+        for c in range(2):
+            fetch_n4(3, c)
+            finish(3, c)
+        nc.scalar.copy(walk_grouped(grouped[0]), walk_planes(res[:, 0]))
+        nc.vector.tensor_copy(walk_grouped(grouped[1]), walk_planes(res[:, 1]))
+        for c in range(2):
+            hand_on(c)
         for q in range(QUADS):
             queue = (nc.sync, nc.scalar)[q % 2]
             queue.dma_start(out_2[0, 4 * q : 4 * q + 4, :].bitcast(I32), out_s[32 * q : 32 * q + 4, :].bitcast(I32))

@@ -20,6 +20,7 @@ PACK = 4
 QUADS = 4
 HALF = S // 2
 SPARE = 16
+SHARE = 160
 
 
 def tile_picked_mixincubeghopm_none_po_kernel(
@@ -85,7 +86,7 @@ def tile_picked_mixincubeghopm_none_po_kernel(
             return planes.rearrange("p t (c i) -> p c t i", i=4)
 
         def walk_grouped(grouped):
-            return grouped[:].rearrange("p (c i) t -> p c t i", i=4)
+            return grouped.rearrange("p (c i) t -> p c t i", i=4)
 
         def quantize(grouped, codes, scales):
             nc.vector.quantize_mx(out=codes.bitcast(FP8X4), scales=scales, in_=grouped[:].rearrange("p j t -> p (j t)"))
@@ -138,10 +139,12 @@ def tile_picked_mixincubeghopm_none_po_kernel(
             nc.scalar.activation(y[t][:], y_ps[t][:], ACT.Copy)
             nc.vector.tensor_tensor(b[:, t, :], tanh_y[t][:].indirect(n2_t[:]), y[t][:], ALU.mult)
 
-        h_ps = [[ps.tile([P, HALF], F32, name=f"h_ps{t}_{c}", tag=("early", "late")[c] + str(t)) for c in range(2)] for t in range(PACK)]
+        h0_ps = [ps.tile([P, HALF], F32, name=f"h0_ps{c}", tag=("early0", "late0")[c]) for c in range(2)]
+        h_ps = {t: ps.tile([P, S], F32, name=f"h_ps{t}", tag=f"early{t}") for t in range(1, PACK)}
         for c in range(2):
-            for t in range(PACK):
-                mm(h_ps[t][c][:], w3, w32s, 0, t, x2[:, cols(c)], x2_s[:, cols(c)], True, False)
+            mm(h0_ps[c][:], w3, w32s, 0, 0, x2[:, cols(c)], x2_s[:, cols(c)], True, False)
+        for t in range(1, PACK):
+            mm(h_ps[t][:], w3, w32s, 0, t, x2[:], x2_s[:], True, False)
 
         z = [sb.tile([P, PACK, HALF], F32, name=f"z{c}") for c in range(2)]
         z_grouped = [sb.tile([P, HALF, PACK], BF16, name=f"z_grouped{c}", align_bytes=64) for c in range(2)]
@@ -152,14 +155,15 @@ def tile_picked_mixincubeghopm_none_po_kernel(
             nc.vector.scalar_tensor_tensor(z[c][:, t, :], b[:, t, cols(c)], gain[:, t : t + 1], y_n1[:], ALU.mult, ALU.mult)
 
         def round_z(c):
-            nc.vector.tensor_copy(walk_grouped(z_grouped[c]), walk_planes(z[c][:]))
+            nc.vector.tensor_copy(walk_grouped(z_grouped[c][:]), walk_planes(z[c][:]))
 
         def second_product(c):
             zq = sb.tile([P, HALF], U32, name=f"zq{c}", align_bytes=64)
             zq_s = sb.tile([P, HALF], U8, name=f"zq_s{c}", align_bytes=64)
             quantize(z_grouped[c], zq[:], zq_s[:])
-            for t in range(PACK):
-                mm(h_ps[t][c][:], w2, w32s, 4, t, zq[:], zq_s[:], False, True)
+            mm(h0_ps[c][:], w2, w32s, 4, 0, zq[:], zq_s[:], False, True)
+            for t in range(1, PACK):
+                mm(h_ps[t][:, cols(c)], w2, w32s, 4, t, zq[:], zq_s[:], False, c == 1)
 
         for t in range(PACK):
             make_z(t, 0)
@@ -169,13 +173,12 @@ def tile_picked_mixincubeghopm_none_po_kernel(
         second_product(0)
         make_z(2, 1)
         make_z(3, 1)
-        for t in range(PACK):
-            nc.scalar.activation(h[t][:, cols(0)], h_ps[t][0][:], ACT.Copy)
+        nc.scalar.activation(h[0][:, cols(0)], h0_ps[0][:], ACT.Copy)
         round_z(1)
         second_product(1)
-        nc.scalar.activation(h[0][:, cols(1)], h_ps[0][1][:], ACT.Copy)
+        nc.scalar.activation(h[0][:, cols(1)], h0_ps[1][:], ACT.Copy)
         for t in range(1, PACK):
-            nc.vector.tensor_copy(h[t][:, cols(1)], h_ps[t][1][:])
+            nc.vector.tensor_copy(h[t][:, :S], h_ps[t][:])
 
         res = sb.tile([P, 2, PACK, HALF], F32, name="res")
         st = [sb.tile([P, S], F32, name=f"st{t}") for t in range(PACK)]
@@ -245,9 +248,10 @@ def tile_picked_mixincubeghopm_none_po_kernel(
         finish_whole(2)
         for c in range(2):
             fetch_n4(3, c)
+        for c in range(2):
             finish(3, c)
-        nc.scalar.copy(walk_grouped(grouped[0]), walk_planes(res[:, 0]))
-        nc.vector.tensor_copy(walk_grouped(grouped[1]), walk_planes(res[:, 1]))
+            nc.vector.tensor_copy(walk_grouped(grouped[c][:, :SHARE]), walk_planes(res[:, c, :, :SHARE]))
+            nc.scalar.copy(walk_grouped(grouped[c][:, SHARE:]), walk_planes(res[:, c, :, SHARE:]))
         for c in range(2):
             hand_on(c)
         for q in range(QUADS):

@@ -58,9 +58,9 @@ def tile_picked_mixincubeghopm_none_po_kernel(
                     nc.sync.dma_start(tile[32 * q + k : 32 * q + k + 4, :].bitcast(I32), rows)
             return tile
 
-        def deal(raw, name, view):
+        def deal(engine, raw, name, view):
             tile = sb.tile([P, raw.shape[1]], raw.dtype, name=name, align_bytes=64)
-            nc.vector.tensor_copy(
+            engine.tensor_copy(
                 tile[:].bitcast(view).rearrange("p (t c i) -> p c t i", t=PACK, i=4),
                 raw[:].bitcast(view).rearrange("p (c i t) -> p c t i", t=PACK, i=4),
             )
@@ -112,9 +112,9 @@ def tile_picked_mixincubeghopm_none_po_kernel(
 
         xq_s = gather_tokens(xs, offs_t, U8, "xq_s")
         x2_s = gather_tokens(xs, two_t, U8, "x2_s")
-        w1s = deal(w1s_raw, "w1s", U8)
+        w1s = deal(nc.gpsimd, w1s_raw, "w1s", U8)
         xq = gather_tokens(xw, offs_t, U32, "xq")
-        w1 = deal(w1_raw, "w1", I32)
+        w1 = deal(nc.gpsimd, w1_raw, "w1", I32)
 
         def mm(out, w, ws, k, t, rhs, rhs_s, start, stop):
             m = slice(t * P, (t + 1) * P)
@@ -123,24 +123,32 @@ def tile_picked_mixincubeghopm_none_po_kernel(
                 rhs=rhs.bitcast(FP8X4), rhs_scale=rhs_s, start=start, stop=stop,
             )
 
-        y_ps = [ps.tile([P, S], F32, name=f"y_ps{t}", tag=f"late{t}") for t in range(PACK)]
-        for t in range(PACK):
+        y0_ps = [ps.tile([P, HALF], F32, name=f"y0_ps{c}", tag=f"bank{c}") for c in range(2)]
+        y_ps = {t: ps.tile([P, S], F32, name=f"y_ps{t}", tag=f"bank{t + 1}") for t in range(1, PACK)}
+        for c in range(2):
+            mm(y0_ps[c][:], w1, w1s, 0, 0, xq[:, cols(c)], xq_s[:, cols(c)], True, True)
+        for t in range(1, PACK):
             mm(y_ps[t][:], w1, w1s, 0, t, xq[:], xq_s[:], True, True)
 
-        x2 = gather_tokens(xw, two_t, U32, "x2", tag="w1_raw")
-        w3 = deal(w3_raw, "w3", I32)
-        w2 = deal(w2_raw, "w2", I32)
-        w32s = deal(w32s_raw, "w32s", U8)
+        x2 = gather_tokens(xw, two_t, U32, "x2")
+        w3 = deal(nc.gpsimd, w3_raw, "w3", I32)
+        w2 = deal(nc.gpsimd, w2_raw, "w2", I32)
+        w32s = deal(nc.vector, w32s_raw, "w32s", U8)
 
         y = [sb.tile([P, S], F32, name=f"y{t}") for t in range(PACK)]
         b = sb.tile([P, PACK, S], F32, name="b")
         for t in range(PACK):
-            nc.scalar.activation(tanh_y[t][:, :S], y_ps[t][:], ACT.Tanh)
-            nc.scalar.activation(y[t][:], y_ps[t][:], ACT.Copy)
+            if t == 0:
+                for c in range(2):
+                    nc.scalar.activation(tanh_y[0][:, cols(c)], y0_ps[c][:], ACT.Tanh)
+                    nc.vector.tensor_copy(y[0][:, cols(1 - c)], y0_ps[1 - c][:])
+            else:
+                nc.scalar.activation(tanh_y[t][:, :S], y_ps[t][:], ACT.Tanh)
+                nc.scalar.activation(y[t][:], y_ps[t][:], ACT.Copy)
             nc.vector.tensor_tensor(b[:, t, :], tanh_y[t][:].indirect(n2_t[:]), y[t][:], ALU.mult)
 
-        h0_ps = [ps.tile([P, HALF], F32, name=f"h0_ps{c}", tag=("early0", "late0")[c]) for c in range(2)]
-        h_ps = {t: ps.tile([P, S], F32, name=f"h_ps{t}", tag=f"early{t}") for t in range(1, PACK)}
+        h0_ps = [ps.tile([P, HALF], F32, name=f"h0_ps{c}", tag=f"bank{c}") for c in range(2)]
+        h_ps = {t: ps.tile([P, S], F32, name=f"h_ps{t}", tag=f"bank{t + 4}") for t in range(1, PACK)}
         for c in range(2):
             mm(h0_ps[c][:], w3, w32s, 0, 0, x2[:, cols(c)], x2_s[:, cols(c)], True, False)
         for t in range(1, PACK):

from contextlib import ExitStack

import concourse.mybir as mybir

K, T, S, H, N = 512, 2048, 512, 512, 512
FLOPS = 2 * S * (K * H + H * N + K * N)

F32 = mybir.dt.float32
BF16 = mybir.dt.bfloat16
I32 = mybir.dt.int32
U32 = mybir.dt.uint32
U16 = mybir.dt.uint16
U8 = mybir.dt.uint8
FP8X4 = mybir.dt.float8_e4m3fn_x4
ALU = mybir.AluOpType
ACT = mybir.ActivationFunctionType

P = 128
PACK = 4
QUADS = 4
HALF = S // 2
SPARE = 16
SHARE = 160


def tile_picked_mixincubeghopm_none_po_kernel(
    tc, x_words, x_scales, w1_words, w1_scales, gn, w2_words, w2_scales, w3_words, w3_scales,
    offs, n1, n2, two, n3, n4, out_0, out_1, out_2,
):
    nc = tc.nc
    with ExitStack() as ctx:
        sb = ctx.enter_context(tc.tile_pool(name="sb", bufs=1))
        ps = ctx.enter_context(tc.psum_pool(name="ps", bufs=1))

        def load_list(src, name):
            tile = sb.tile(list(src.shape), U16, name=name)
            nc.sync.dma_start(tile[:], src)
            return tile

        def load_words(src, name, queue):
            tile = sb.tile([P, src.shape[2]], U32, name=name, tag=name, align_bytes=64)
            queue.dma_start(tile[:].bitcast(I32), src[0].rearrange("p n t -> p (n t)").bitcast(I32))
            return tile

        def load_scales(src, name, queues):
            tile = sb.tile([P, src.shape[2]], U8, name=name, align_bytes=64)
            for q in range(QUADS):
                rows = src[0, 4 * q : 4 * q + 4, :].bitcast(I32)
                queues[q].dma_start(tile[32 * q : 32 * q + 32, :].bitcast(I32), rows.partition_broadcast(8))
            return tile

        def load_scale_pair(first, second, name):
            tile = sb.tile([P, first.shape[2]], U8, name=name, align_bytes=64)
            nc.gpsimd.memset(tile[:].bitcast(I32), 0)
            for k, src in ((0, first), (4, second)):
                for q in range(QUADS):
                    rows = src[0, 4 * q : 4 * q + 4, :].bitcast(I32)
                    nc.sync.dma_start(tile[32 * q + k : 32 * q + k + 4, :].bitcast(I32), rows)
            return tile

        def deal(engine, raw, name, view):
            tile = sb.tile([P, raw.shape[1]], raw.dtype, name=name, align_bytes=64)
            engine.tensor_copy(
                tile[:].bitcast(view).rearrange("p (t c i) -> p c t i", t=PACK, i=4),
                raw[:].bitcast(view).rearrange("p (c i t) -> p c t i", t=PACK, i=4),
            )
            return tile

        def gather_tokens(table, lst, dtype, name, tag=None):
            tile = sb.tile([P, S], dtype, name=name, tag=tag or name, align_bytes=64)
            nc.vector.tensor_copy(tile[:], table[:].indirect(lst[:]))
            return tile

        def window(name):
            tile = sb.tile([P, S + SPARE], F32, name=name)
            nc.gpsimd.memset(tile[:, S:], 0.0)
            return tile

        def cols(c):
            return slice(c * HALF, (c + 1) * HALF)

        def entries(lst, piece, count):
            return lst[:, piece * count // 16 : (piece + 1) * count // 16]

        def walk_planes(planes):
            return planes.rearrange("p t (c i) -> p c t i", i=4)

        def walk_grouped(grouped):
            return grouped.rearrange("p (c i) t -> p c t i", i=4)

        def quantize(grouped, codes, scales):
            nc.vector.quantize_mx(out=codes.bitcast(FP8X4), scales=scales, in_=grouped[:].rearrange("p j t -> p (j t)"))

        offs_t = load_list(offs, "offs_t")
        two_t = load_list(two, "two_t")
        xs = load_scales(x_scales, "xs", (nc.scalar, nc.scalar, nc.scalar, nc.sync))
        xw = load_words(x_words, "xw", nc.scalar)
        w1s_raw = load_scales(w1_scales, "w1s_raw", (nc.sync,) * QUADS)
        w1_raw = load_words(w1_words, "w1_raw", nc.sync)
        n2_t = load_list(n2, "n2_t")
        n1_t = load_list(n1, "n1_t")
        gain = sb.tile([P, PACK], F32, name="gain")
        nc.sync.dma_start(gain[:], gn.rearrange("(p t) o -> p (t o)", t=PACK))
        w3_raw = load_words(w3_words, "w3_raw", nc.sync)
        w2_raw = load_words(w2_words, "w2_raw", nc.sync)
        w32s_raw = load_scale_pair(w3_scales, w2_scales, "w32s_raw")
        n3_t = load_list(n3, "n3_t")
        n4_t = load_list(n4, "n4_t")

        tanh_y = [window(f"tanh_y{t}") for t in range(PACK)]
        h = [window(f"h{t}") for t in range(PACK)]

        xq_s = gather_tokens(xs, offs_t, U8, "xq_s")
        x2_s = gather_tokens(xs, two_t, U8, "x2_s")
        w1s = deal(nc.gpsimd, w1s_raw, "w1s", U8)
        xq = gather_tokens(xw, offs_t, U32, "xq")
        w1 = deal(nc.gpsimd, w1_raw, "w1", I32)

        def mm(out, w, ws, k, t, rhs, rhs_s, start, stop):
            m = slice(t * P, (t + 1) * P)
            nc.tensor.matmul_mx(
                out=out, lhsT=w[:, m].bitcast(FP8X4), lhsT_scale=ws[k:, m],
                rhs=rhs.bitcast(FP8X4), rhs_scale=rhs_s, start=start, stop=stop,
            )

        y0_ps = [ps.tile([P, HALF], F32, name=f"y0_ps{c}", tag=f"bank{c}") for c in range(2)]
        y_ps = {t: ps.tile([P, S], F32, name=f"y_ps{t}", tag=f"bank{t + 1}") for t in range(1, PACK)}
        for c in range(2):
            mm(y0_ps[c][:], w1, w1s, 0, 0, xq[:, cols(c)], xq_s[:, cols(c)], True, True)
        for t in range(1, PACK):
            mm(y_ps[t][:], w1, w1s, 0, t, xq[:], xq_s[:], True, True)

        x2 = gather_tokens(xw, two_t, U32, "x2")
        w3 = deal(nc.gpsimd, w3_raw, "w3", I32)
        w2 = deal(nc.gpsimd, w2_raw, "w2", I32)
        w32s = deal(nc.vector, w32s_raw, "w32s", U8)

        y = [sb.tile([P, S], F32, name=f"y{t}") for t in range(PACK)]
        b = sb.tile([P, PACK, S], F32, name="b")
        for t in range(PACK):
            if t == 0:
                for c in range(2):
                    nc.scalar.activation(tanh_y[0][:, cols(c)], y0_ps[c][:], ACT.Tanh)
                    nc.vector.tensor_copy(y[0][:, cols(1 - c)], y0_ps[1 - c][:])
            else:
                nc.scalar.activation(tanh_y[t][:, :S], y_ps[t][:], ACT.Tanh)
                nc.scalar.activation(y[t][:], y_ps[t][:], ACT.Copy)
            nc.vector.tensor_tensor(b[:, t, :], tanh_y[t][:].indirect(n2_t[:]), y[t][:], ALU.mult)

        h0_ps = [ps.tile([P, HALF], F32, name=f"h0_ps{c}", tag=f"bank{c}") for c in range(2)]
        h_ps = {t: ps.tile([P, S], F32, name=f"h_ps{t}", tag=f"bank{t + 4}") for t in range(1, PACK)}
        for c in range(2):
            mm(h0_ps[c][:], w3, w32s, 0, 0, x2[:, cols(c)], x2_s[:, cols(c)], True, False)
        for t in range(1, PACK):
            mm(h_ps[t][:], w3, w32s, 0, t, x2[:], x2_s[:], True, False)

        z = [sb.tile([P, PACK, HALF], F32, name=f"z{c}") for c in range(2)]
        z_grouped = [sb.tile([P, HALF, PACK], BF16, name=f"z_grouped{c}", align_bytes=64) for c in range(2)]

        def make_z(t, c):
            y_n1 = sb.tile([P, HALF], F32, name=f"y_n1_{t}_{c}")
            nc.scalar.activation(y_n1[:], y[t][:].indirect(entries(n1_t, c, HALF)), ACT.Copy)
            nc.vector.scalar_tensor_tensor(z[c][:, t, :], b[:, t, cols(c)], gain[:, t : t + 1], y_n1[:], ALU.mult, ALU.mult)

        def round_z(c):
            nc.vector.tensor_copy(walk_grouped(z_grouped[c][:]), walk_planes(z[c][:]))

        def second_product(c):
            zq = sb.tile([P, HALF], U32, name=f"zq{c}", align_bytes=64)
            zq_s = sb.tile([P, HALF], U8, name=f"zq_s{c}", align_bytes=64)
            quantize(z_grouped[c], zq[:], zq_s[:])
            mm(h0_ps[c][:], w2, w32s, 4, 0, zq[:], zq_s[:], False, True)
            for t in range(1, PACK):
                mm(h_ps[t][:, cols(c)], w2, w32s, 4, t, zq[:], zq_s[:], False, c == 1)

        for t in range(PACK):
            make_z(t, 0)
        make_z(0, 1)
        round_z(0)
        make_z(1, 1)
        second_product(0)
        make_z(2, 1)
        make_z(3, 1)
        nc.scalar.activation(h[0][:, cols(0)], h0_ps[0][:], ACT.Copy)
        round_z(1)
        second_product(1)
        nc.scalar.activation(h[0][:, cols(1)], h0_ps[1][:], ACT.Copy)
        for t in range(1, PACK):
            nc.vector.tensor_copy(h[t][:, :S], h_ps[t][:])

        res = sb.tile([P, 2, PACK, HALF], F32, name="res")
        st = [sb.tile([P, S], F32, name=f"st{t}") for t in range(PACK)]
        st_n4 = [sb.tile([P, S], F32, name=f"st_n4_{t}") for t in range(PACK)]
        mx = [[sb.tile([P, HALF], F32, name=f"mx{t}_{c}") for c in range(2)] for t in range(PACK)]
        out_rows = out_0.rearrange("(p t) (c j) -> p c t j", t=PACK, c=2)

        def members(t, c):
            mb = sb.tile([P, HALF, 2], F32, name=f"mb{t}_{c}")
            nc.scalar.activation(mb[:].rearrange("p j m -> p (j m)"), h[t][:].indirect(entries(n3_t, c, S)), ACT.Copy)
            nc.vector.tensor_tensor(mx[t][c][:], mb[:, :, 0], mb[:, :, 1], ALU.max)

        def subtract(t, c):
            nc.vector.tensor_tensor(st[t][:, cols(c)], h[t][:, cols(c)], mx[t][c][:], ALU.subtract)

        def fetch_n4(t, c):
            looked_up = st[t][:].indirect(entries(n4_t, c, HALF))
            if t < 2:
                nc.vector.tensor_copy(st_n4[t][:, cols(c)], looked_up)
            else:
                nc.scalar.activation(st_n4[t][:, cols(c)], looked_up, ACT.Copy)

        def finish(t, c):
            nc.vector.tensor_tensor(res[:, c, t, :], st[t][:, cols(c)], st_n4[t][:, cols(c)], ALU.max)
            if c == 1 or t == 3:
                halves = slice(c, c + 1) if t == 3 else slice(0, 2)
                nc.sync.dma_start(out_rows[:, halves, t, :], res[:, halves, t, :])

        def finish_whole(t):
            halves = "p (c j) -> p c j"
            nc.vector.tensor_tensor(res[:, :, t, :], st[t][:].rearrange(halves, c=2), st_n4[t][:].rearrange(halves, c=2), ALU.max)
            nc.sync.dma_start(out_rows[:, :, t, :], res[:, :, t, :])

        out_s = sb.tile([P, S], U8, name="out_s", align_bytes=64)
        grouped = [sb.tile([P, HALF, PACK], BF16, name=f"res_grouped{c}", align_bytes=64) for c in range(2)]
        codes = [sb.tile([P, HALF], U32, name=f"out_w{c}", align_bytes=64) for c in range(2)]
        words = out_1[0].rearrange("p n t -> p (n t)").bitcast(I32)

        def hand_on(c):
            quantize(grouped[c], codes[c][:], out_s[:, cols(c)])
            nc.sync.dma_start(words[:, cols(c)], codes[c][:].bitcast(I32))

        for c in range(2):
            members(0, c)
            subtract(0, c)
        fetch_n4(0, 0)
        members(1, 0)
        fetch_n4(0, 1)
        subtract(1, 0)
        members(1, 1)
        finish_whole(0)
        subtract(1, 1)
        members(2, 0)
        fetch_n4(1, 0)
        subtract(2, 0)
        fetch_n4(1, 1)
        members(2, 1)
        members(3, 0)
        subtract(2, 1)
        subtract(3, 0)
        members(3, 1)
        finish(1, 0)
        subtract(3, 1)
        finish(1, 1)
        for c in range(2):
            fetch_n4(2, c)
        finish_whole(2)
        for c in range(2):
            fetch_n4(3, c)
        for c in range(2):
            finish(3, c)
            nc.vector.tensor_copy(walk_grouped(grouped[c][:, :SHARE]), walk_planes(res[:, c, :, :SHARE]))
            nc.scalar.copy(walk_grouped(grouped[c][:, SHARE:]), walk_planes(res[:, c, :, SHARE:]))
        for c in range(2):
            hand_on(c)
        for q in range(QUADS):
            queue = (nc.sync, nc.scalar)[q % 2]
            queue.dma_start(out_2[0, 4 * q : 4 * q + 4, :].bitcast(I32), out_s[32 * q : 32 * q + 4, :].bitcast(I32))
